import numpy as np
import ml_dtypes

BF16 = ml_dtypes.bfloat16


def bf(x):
    return np.asarray(x, np.float32).astype(BF16)


def f32(x):
    return np.asarray(x, np.float32)


def f64(x):
    return np.asarray(x).astype(np.float64)


def striped(idx):
    return np.tile(idx.reshape(-1, 16).T, (8, 1))


S, K, M, N, E, Q = 512, 128, 128, 1024, 4, 256


def two_experts():
    first = np.random.permutation(S).reshape(E, S // E)
    return np.concatenate([np.random.permutation(np.concatenate([first[e], first[(e + 1) % E]])) for e in range(E)])


def setup_inputs():
    return {"table": bf(np.random.standard_normal((S, K))), "w": bf(np.random.standard_normal((E, K, M)) / np.sqrt(K)), "c": f32(0.2 + 0.8 * np.random.random_sample((1, N))), "offs": striped(two_experts())}


def reference(table, w, c, offs):
    idx = offs[:16].T.reshape(-1)
    x = f64(table)[idx].T
    y = np.concatenate([f64(w)[e].T @ x[:, e * Q : (e + 1) * Q] for e in range(E)], axis=1)
    return y * f64(c)

@@ -1,0 +1,48 @@
+import concourse.mybir as mybir
+from concourse.masks import make_identity
+
+BF16, F32, U16 = mybir.dt.bfloat16, mybir.dt.float32, mybir.dt.uint16
+
+FLOPS = 2 * 128 * 128 * 1024 + 128 * 1024
+
+
+def tile_gather_matmul_kernel(tc, table, w, c, offs, out):
+    nc = tc.nc
+    tokens, features = table.shape
+    experts, out_features = w.shape[0], w.shape[2]
+    entries = c.shape[1]
+    piece = entries // experts
+    offset_columns = piece // 16
+    blocks = tokens // 128
+
+    with (
+        tc.tile_pool(name="held", bufs=1) as held,
+        tc.psum_pool(name="flip_psum", bufs=1) as flip_psum,
+        tc.psum_pool(name="product_psum", bufs=experts) as product_psum,
+    ):
+        token_rows = held.tile([128, blocks, features], BF16)
+        nc.sync.dma_start(token_rows[:], table.rearrange("(a p) k -> p a k", p=128))
+        weights = held.tile([features, experts, out_features], BF16)
+        nc.scalar.dma_start(weights[:], w.rearrange("e k m -> k e m"))
+        offsets = held.tile([128, entries // 16], U16)
+        nc.sync.dma_start(offsets[:], offs)
+        factors = held.tile([out_features, entries], F32)
+        nc.scalar.dma_start(factors[:], c.partition_broadcast(128))
+
+        identity = held.tile([128, 128], BF16)
+        make_identity(nc, identity[:])
+
+        flipped = flip_psum.tile([features, tokens], BF16)
+        for a in range(blocks):
+            nc.tensor.transpose(flipped[:, a * 128 : (a + 1) * 128], token_rows[:, a, :], identity[:])
+        token_columns = held.tile([features, tokens], BF16)
+        nc.vector.tensor_copy(token_columns[:], flipped[:])
+
+        scaled = held.tile([out_features, entries], F32)
+        for e in range(experts):
+            columns = slice(e * piece, (e + 1) * piece)
+            picked = token_columns[:].indirect(offsets[:, e * offset_columns : (e + 1) * offset_columns])
+            product = product_psum.tile([out_features, piece], F32)
+            nc.tensor.matmul(product[:], weights[:, e, :], picked, start=True, stop=True)
+            nc.vector.tensor_tensor(scaled[:, columns], product[:], factors[:, columns], mybir.AluOpType.mult)
+            nc.sync.dma_start(out[:, columns], scaled[:, columns])

@@ -22,12 +22,12 @@ def tile_gather_matmul_kernel(tc, table, w, c, offs, out):
     ):
         token_rows = held.tile([128, blocks, features], BF16)
         nc.sync.dma_start(token_rows[:], table.rearrange("(a p) k -> p a k", p=128))
-        weights = held.tile([features, experts, out_features], BF16)
-        nc.scalar.dma_start(weights[:], w.rearrange("e k m -> k e m"))
         offsets = held.tile([128, entries // 16], U16)
         nc.sync.dma_start(offsets[:], offs)
+        weights = held.tile([features, experts, out_features], BF16)
+        nc.sync.dma_start(weights[:], w.rearrange("e k m -> k e m"))
         factors = held.tile([out_features, entries], F32)
-        nc.scalar.dma_start(factors[:], c.partition_broadcast(128))
+        nc.sync.dma_start(factors[:], c.partition_broadcast(128))
 
         identity = held.tile([128, 128], BF16)
         make_identity(nc, identity[:])

import concourse.mybir as mybir
from concourse.masks import make_identity

BF16, F32, U16 = mybir.dt.bfloat16, mybir.dt.float32, mybir.dt.uint16

FLOPS = 2 * 128 * 128 * 1024 + 128 * 1024


def tile_gather_matmul_kernel(tc, table, w, c, offs, out):
    nc = tc.nc
    tokens, features = table.shape
    experts, out_features = w.shape[0], w.shape[2]
    entries = c.shape[1]
    piece = entries // experts
    offset_columns = piece // 16
    blocks = tokens // 128

    with (
        tc.tile_pool(name="held", bufs=1) as held,
        tc.psum_pool(name="flip_psum", bufs=1) as flip_psum,
        tc.psum_pool(name="product_psum", bufs=experts) as product_psum,
    ):
        token_rows = held.tile([128, blocks, features], BF16)
        nc.sync.dma_start(token_rows[:], table.rearrange("(a p) k -> p a k", p=128))
        offsets = held.tile([128, entries // 16], U16)
        nc.sync.dma_start(offsets[:], offs)
        weights = held.tile([features, experts, out_features], BF16)
        nc.sync.dma_start(weights[:], w.rearrange("e k m -> k e m"))
        factors = held.tile([out_features, entries], F32)
        nc.sync.dma_start(factors[:], c.partition_broadcast(128))

        identity = held.tile([128, 128], BF16)
        make_identity(nc, identity[:])

        flipped = flip_psum.tile([features, tokens], BF16)
        for a in range(blocks):
            nc.tensor.transpose(flipped[:, a * 128 : (a + 1) * 128], token_rows[:, a, :], identity[:])
        token_columns = held.tile([features, tokens], BF16)
        nc.vector.tensor_copy(token_columns[:], flipped[:])

        scaled = held.tile([out_features, entries], F32)
        for e in range(experts):
            columns = slice(e * piece, (e + 1) * piece)
            picked = token_columns[:].indirect(offsets[:, e * offset_columns : (e + 1) * offset_columns])
            product = product_psum.tile([out_features, piece], F32)
            nc.tensor.matmul(product[:], weights[:, e, :], picked, start=True, stop=True)
            nc.vector.tensor_tensor(scaled[:, columns], product[:], factors[:, columns], mybir.AluOpType.mult)
            nc.sync.dma_start(out[:, columns], scaled[:, columns])
